import numpy as np
import ml_dtypes


def mxq(x, axis, fmt="e4m3"):
    dtype, down = {"e4m3": (ml_dtypes.float8_e4m3fn, 7), "e5m2": (ml_dtypes.float8_e5m2, 14)}[fmt]
    v = np.moveaxis(np.asarray(x, np.float32).astype(ml_dtypes.bfloat16).astype(np.float64), axis, -1)
    blocks = v.reshape(v.shape[:-1] + (-1, 32))
    amax = np.abs(blocks).max(-1, keepdims=True)
    byte = np.maximum(np.where(amax > 0, np.frexp(amax)[1] - 1 + 127, 0) - down, 1)
    scale = np.exp2(byte - 127.0)
    codes = (blocks / scale).astype(np.float32).astype(dtype).astype(np.float64)
    return np.moveaxis((codes * scale).reshape(v.shape), -1, axis)


WIDE = False


def mx_kscale(k):
    if not WIDE:
        return np.ones(k)
    levels = np.array([10, -10, 5, -5, 0])
    if k % 512:
        return np.exp2(np.random.permutation(np.resize(levels, k // 32))).repeat(32)
    a = np.empty((k // 512, 16))
    for p in range(k // 512):
        a[p, :8] = np.random.permutation(np.resize(levels, 8))
        for g in range(8):
            far = levels[np.abs(levels - a[p, g]) >= 10]
            a[p, g + 8] = far[np.random.randint(len(far))]
    return np.exp2(a.ravel()).repeat(32)


def f64(x):
    return np.asarray(x).astype(np.float64)


E2M1 = np.array([0.0, 0.5, 1.0, 1.5, 2.0, 3.0, 4.0, 6.0, -0.0, -0.5, -1.0, -1.5, -2.0, -3.0, -4.0, -6.0])


def pack_weight(w, fmt):
    k, n = w.shape
    w = f64(np.asarray(w, np.float32).astype(ml_dtypes.bfloat16)).reshape(k // 32, 32, n)
    amax = np.abs(w).max(1)
    if fmt == "e4m3":
        byte = np.frexp(amax)[1] - 1 + 127 - 7
    else:
        mant, ex = np.frexp(amax / 6.0)
        byte = np.where(mant > 0.5, ex, ex - 1) + 127
    byte = np.clip(np.where(amax > 0, byte, 1), 1, 254)
    scaled = (w * np.exp2(127.0 - byte)[:, None, :]).reshape(k, n).astype(np.float32)
    by_word = np.ascontiguousarray(scaled.reshape(k // 512, 128, 4, n).transpose(0, 1, 3, 2))
    if fmt == "e4m3":
        words = by_word.astype(ml_dtypes.float8_e4m3fn).view(np.uint8)
    else:
        c = by_word.astype(ml_dtypes.float4_e2m1fn).view(np.uint8) & 0xF
        words = (c[..., 0::2] | (c[..., 1::2] << 4)).reshape(k // 512, 128, 2 * n)
    return np.ascontiguousarray(words), np.ascontiguousarray(byte.astype(np.uint8).reshape(k // 512, 16, n))


def unpack_weight(words, scales, fmt):
    g, _, n = scales.shape
    words = np.ascontiguousarray(words).reshape(g, 128, n, -1)
    if fmt == "e4m3":
        vals = words.view(ml_dtypes.float8_e4m3fn).astype(np.float64)
    else:
        nib = np.empty((g, 128, n, 4), np.uint8)
        nib[..., 0::2] = words & 0xF
        nib[..., 1::2] = words >> 4
        vals = E2M1[nib]
    vals = vals * np.repeat(np.exp2(scales.astype(np.float64) - 127.0), 8, axis=1)[..., None]
    return vals.transpose(0, 1, 3, 2).reshape(g * 512, n)


def planes(y):
    n, m = y.shape
    v = y.astype(np.float32).astype(ml_dtypes.bfloat16).astype(np.float64).reshape(n // 32, 32, m)
    top = np.abs(v).max(1)
    byte = np.clip(np.where(top > 0, np.frexp(top)[1] - 1 + 127 - 7, 1), 1, 254)
    codes = (v * np.exp2(127.0 - byte)[:, None, :]).reshape(n, m).astype(np.float32).astype(ml_dtypes.float8_e4m3fn).view(np.uint8)
    words = codes.reshape(n // 512, 128, 4, m).transpose(0, 1, 3, 2)
    return np.ascontiguousarray(words), np.ascontiguousarray(byte.astype(np.uint8).reshape(n // 512, 16, m))


def gelu(v):
    return 0.5 * v * (1.0 + np.tanh(np.sqrt(2.0 / np.pi) * (v + 0.044715 * v**3)))


K, M, T = 512, 1024, 1024


def setup_inputs():
    n = np.random.standard_normal
    s = mx_kscale(K)[:, None]
    u = mx_kscale(T)[:, None]
    q = n((K, T)) * s
    p_vc = pack_weight(0.1 * n((T, M)) / u, "e2m1")
    return {
        "qc": (q).astype(np.float32),
        "kc": (n((K, T)) / np.sqrt(K) / s).astype(np.float32),
        "qd": (q * 0.995 ** (np.arange(T) + 1.0)).astype(np.float32),
        "st": (n((K, M)) / np.sqrt(K) / s).astype(np.float32),
        "vc_words": p_vc[0],
        "vc_scales": p_vc[1],
        "dm": (np.tril(0.995 ** (np.arange(T)[:, None] - np.arange(T)[None])).T * u).astype(np.float32),
        "b": (0.3 * n(1024)).astype(np.float32),
    }


def reference(qc, kc, qd, st, vc_words, vc_scales, dm, b):
    qc_ = mxq(f64(qc), 0, "e4m3")
    kc_ = mxq(f64(kc), 0, "e4m3")
    qd_ = mxq(f64(qd), 0, "e4m3")
    st_ = mxq(f64(st), 0, "e4m3")
    vc_ = unpack_weight(vc_words, vc_scales, "e2m1")
    h_ = mxq((kc_.T @ qc_) * f64(dm), 0, "e4m3")
    y = h_.T @ vc_ + qd_.T @ st_
    out_0 = gelu(y + f64(b)[None, :])
    return (out_0,) + planes(out_0)

@@ -1,0 +1,320 @@
+from contextlib import ExitStack
+
+import concourse.mybir as mybir
+from concourse.masks import make_identity
+
+K, M, T = 512, 1024, 1024
+FLOPS = 2 * K * T * T + 2 * T * T * M + 2 * K * T * M
+
+F32 = mybir.dt.float32
+BF16 = mybir.dt.bfloat16
+I32 = mybir.dt.int32
+U32 = mybir.dt.uint32
+U8 = mybir.dt.uint8
+E4M3 = mybir.dt.float8_e4m3fn_x4
+E2M1 = mybir.dt.float4_e2m1fn_x4
+GELU = mybir.ActivationFunctionType.Gelu_apprx_tanh
+
+P = 128
+W = 512
+HALF = 256
+
+
+def tile_mix_linattn_tm_pl_gelu_kernel(tc, qc, kc, qd, st, vc_words, vc_scales, dm, b, out_0, out_1, out_2):
+    nc = tc.nc
+    V, S = nc.vector, nc.scalar
+    with ExitStack() as ctx:
+        keep = ctx.enter_context(tc.tile_pool(name="keep", bufs=1))
+        stage = ctx.enter_context(tc.tile_pool(name="stage", bufs=10))
+        psum = ctx.enter_context(tc.psum_pool(name="psum", bufs=1))
+        ctx.enter_context(tc.manual_schedule())
+
+        def bank(tag):
+            return psum.tile([P, W], F32, name=tag, tag=tag, bufs={"h": 3, "y": 5}[tag])
+
+        raw = {}
+
+        def load(name, rows):
+            raw[name] = keep.tile([P, 4, W], F32, name="raw_" + name, tag="raw_" + name)
+            nc.sync.dma_start(out=raw[name][:], in_=rows.rearrange("(p j) w -> p j w", j=4))
+
+        vc_codes = {}
+
+        def load_vc(a):
+            vc_codes[a] = keep.tile([P, 2 * M], U8, name="vc%d" % a, tag="vc%d" % a, align_bytes=64)
+            nc.sync.dma_start(out=vc_codes[a][:].bitcast(I32), in_=vc_words[a].bitcast(I32))
+
+        lo, hi = slice(0, W), slice(W, 2 * W)
+        vc_plane = keep.tile([P, 2 * M], U8, align_bytes=64)
+        V.memset(vc_plane[:].bitcast(I32), 0)
+        warm = keep.tile([P, 8], F32)
+        V.memset(warm[:], 0.0)
+        load("kc0", kc[:, lo])
+        load("qc0", qc[:, lo])
+        b_cols = keep.tile([P, 8], F32)
+        S.dma_start(out=b_cols[:].rearrange("p (h c) -> p h c", h=2), in_=b.rearrange("(h p c) -> p h c", h=2, c=4))
+        for q in range(4):
+            S.dma_start(
+                out=vc_plane[32 * q : 32 * q + 4, :].bitcast(I32).rearrange("p (a w) -> p a w", a=2),
+                in_=vc_scales[:, 4 * q : 4 * q + 4, :].bitcast(I32).rearrange("a r w -> r a w"),
+            )
+        S.activation(out=warm[:], in_=warm[:], func=GELU)
+        load("dm00", dm[lo, lo])
+        load("qd0", qd[:, lo])
+        load_vc(0)
+        load("st0", st[:, lo])
+        load("st1", st[:, hi])
+        load("qc1", qc[:, hi])
+        load("dm01", dm[lo, hi])
+        load("kc1", kc[:, hi])
+        load("qd1", qd[:, hi])
+        load_vc(1)
+        load("dm11", dm[hi, hi])
+
+        ident = keep.tile([P, P], F32)
+        make_identity(nc, ident[:])
+        bias = keep.tile([P, M], F32)
+
+        def spread_bias():
+            for h in range(2):
+                spread = bank("y")
+                for c in range(4):
+                    col = b_cols[:, 4 * h + c : 4 * h + c + 1]
+                    nc.tensor.transpose(spread[:, P * c : P * (c + 1)], col.to_broadcast([P, P]), ident[:])
+                S.copy(
+                    out=bias[:, W * h : W * (h + 1)].rearrange("p (k c) -> p k c", c=4),
+                    in_=spread[:].rearrange("p (c k) -> p k c", c=4),
+                )
+
+        staged, codes, scales = {}, {}, {}
+
+        def staging(name, g):
+            staged[name, g] = stage.tile([P, 4 * HALF], BF16, name="staged", tag="staged", align_bytes=64)
+            return staged[name, g]
+
+        def pairs(tile, g):
+            return tile[:].rearrange("p j (m g s) -> p g m j s", g=2, s=2)[:, g]
+
+        def cast(eng, name, g):
+            dst = staging(name, g)[:]
+            kind = name[:2]
+            if kind in ("kc", "qd"):
+                src, dst = pairs(raw[name], g), dst.rearrange("p (s m j) -> p m j s", s=2, j=4)
+            elif kind == "qc":
+                src, dst = pairs(raw[name], g), dst.rearrange("p (m s j) -> p m j s", s=2, j=4)
+            else:
+                src = raw[name][:, :, HALF * g : HALF * (g + 1)].rearrange("p j (c u) -> p c j u", u=4)
+                dst = dst.rearrange("p (c u j) -> p c j u", u=4, j=4)
+            if eng is V:
+                V.tensor_copy(out=dst, in_=src)
+            else:
+                S.copy(out=dst, in_=src)
+
+        out_plane = keep.tile([P, 2 * M], U8, align_bytes=64)
+
+        def quant(name, g):
+            if name not in codes:
+                codes[name] = keep.tile([P, W], U32, name="c_" + name, tag="c_" + name, align_bytes=64)
+                if name[0] == "o":
+                    at = M * int(name[1]) + W * int(name[2])
+                    scales[name] = out_plane[:, at : at + W]
+                else:
+                    plane = keep.tile([P, W], U8, name="s_" + name, tag="s_" + name, align_bytes=64)
+                    scales[name] = plane[:]
+            cols = slice(HALF * g, HALF * (g + 1))
+            V.quantize_mx(out=codes[name][:, cols].bitcast(E4M3), scales=scales[name][:, cols], in_=staged[name, g][:])
+
+        score_banks = {}
+
+        def scores(ja, ta, g, u):
+            acc = bank("h")
+            score_banks[ja, ta, g, u] = acc
+            kn, qn = "kc%d" % ja, "qc%d" % ta
+            cols = slice(HALF * g + P * u, HALF * g + P * (u + 1))
+            for i in range(4):
+                keys = slice(P * i, P * (i + 1))
+                nc.tensor.matmul_mx(
+                    out=acc[:, keys], lhsT=codes[kn][:, keys].bitcast(E4M3), lhsT_scale=scales[kn][:, keys],
+                    rhs=codes[qn][:, cols].bitcast(E4M3), rhs_scale=scales[qn][:, cols], start=True, stop=True,
+                )
+
+        def decay(ja, ta, g, u):
+            name = "h%d%d" % (ja, ta)
+            if u == 0:
+                staging(name, g)
+            ms = slice(64 * u, 64 * (u + 1))
+            V.tensor_tensor(
+                out=staged[name, g][:].rearrange("p (s m i) -> p m i s", s=2, i=4)[:, ms],
+                in0=score_banks[ja, ta, g, u][:].rearrange("p (i m s) -> p m i s", i=4, s=2),
+                in1=pairs(raw["dm%d%d" % (ja, ta)], g)[:, ms],
+                op=mybir.AluOpType.mult,
+            )
+
+        sums = {}
+
+        def y_pass(a, n, r, part, start=False, stop=False, tag="y"):
+            if start:
+                sums[a, n, r] = bank(tag)
+            rows = slice(P * r, P * (r + 1))
+            if part == "state":
+                left = "qd%d" % a
+                rhs, rhs_scale = codes["st%d" % n][:].bitcast(E4M3), scales["st%d" % n]
+            else:
+                left = "h%d%d" % (part, a)
+                rhs = vc_codes[part][:, 2 * W * n : 2 * W * (n + 1)].bitcast(E2M1)
+                rhs_scale = vc_plane[:, M * part + W * n : M * part + W * (n + 1)]
+            nc.tensor.matmul_mx(
+                out=sums[a, n, r][:], lhsT=codes[left][:, rows].bitcast(E4M3), lhsT_scale=scales[left][:, rows],
+                rhs=rhs, rhs_scale=rhs_scale, start=start, stop=stop,
+            )
+
+        def add_bias(a, n, r):
+            name = "o%d%d" % (a, n)
+            if name not in raw:
+                raw[name] = keep.tile([P, 4, W], F32, name="raw_" + name, tag="raw_" + name)
+            V.tensor_tensor(out=raw[name][:, r, :], in0=sums[a, n, r][:], in1=bias[:, W * n : W * (n + 1)], op=mybir.AluOpType.add)
+
+        def gelu(a, n, r):
+            row = raw["o%d%d" % (a, n)][:, r, :]
+            S.activation(out=row, in_=row, func=GELU)
+
+        def store_values(a, n, rs):
+            dst = out_0[W * a : W * (a + 1), W * n : W * (n + 1)].rearrange("(p r) w -> p r w", r=4)
+            nc.sync.dma_start(out=dst[:, rs, :], in_=raw["o%d%d" % (a, n)][:, rs, :])
+
+        def store_codes(a, n):
+            dst = out_1[a].rearrange("p n t -> p (n t)").bitcast(I32)[:, W * n : W * (n + 1)]
+            nc.sync.dma_start(out=dst, in_=codes["o%d%d" % (a, n)][:].bitcast(I32))
+
+        every = slice(0, 4)
+
+        for name in ("kc0", "qc0"):
+            cast(V, name, 0)
+            cast(S, name, 1)
+            quant(name, 0)
+            quant(name, 1)
+        spread_bias()
+        scores(0, 0, 0, 0)
+        scores(0, 0, 0, 1)
+        scores(0, 0, 1, 0)
+        decay(0, 0, 0, 0)
+        scores(0, 0, 1, 1)
+        decay(0, 0, 0, 1)
+        decay(0, 0, 1, 0)
+        quant("h00", 0)
+        decay(0, 0, 1, 1)
+        cast(S, "qd0", 0)
+        cast(S, "qd0", 1)
+        quant("qd0", 0)
+        quant("h00", 1)
+        quant("qd0", 1)
+        for r in range(4):
+            y_pass(0, 0, r, 0, start=True)
+        cast(V, "st0", 0)
+        cast(S, "st0", 1)
+        quant("st0", 0)
+        quant("st0", 1)
+        for r in range(4):
+            y_pass(0, 0, r, "state", stop=True)
+        cast(S, "st1", 0)
+        cast(S, "st1", 1)
+        y_pass(0, 1, 0, 0, start=True)
+        for r in range(4):
+            add_bias(0, 0, r)
+            gelu(0, 0, r)
+            if r < 3:
+                y_pass(0, 1, r + 1, 0, start=True)
+        store_values(0, 0, every)
+        quant("st1", 0)
+        quant("st1", 1)
+        for r in range(4):
+            y_pass(0, 1, r, "state", stop=True)
+        cast(V, "qc1", 0)
+        cast(S, "qc1", 1)
+        for r in range(4):
+            add_bias(0, 1, r)
+            gelu(0, 1, r)
+            if r == 2:
+                quant("qc1", 0)
+                quant("qc1", 1)
+                scores(0, 1, 0, 0)
+                scores(0, 1, 0, 1)
+                scores(0, 1, 1, 0)
+        store_values(0, 1, every)
+        cast(S, "kc1", 0)
+        cast(S, "kc1", 1)
+        cast(S, "qd1", 0)
+        cast(S, "qd1", 1)
+        decay(0, 1, 0, 0)
+        scores(0, 1, 1, 1)
+        decay(0, 1, 0, 1)
+        decay(0, 1, 1, 0)
+        quant("h01", 0)
+        decay(0, 1, 1, 1)
+        quant("kc1", 0)
+        quant("h01", 1)
+        quant("kc1", 1)
+        scores(1, 1, 0, 0)
+        scores(1, 1, 0, 1)
+        scores(1, 1, 1, 0)
+        for r in range(4):
+            y_pass(1, 0, r, 0, start=True)
+        y_pass(1, 1, 0, 0, start=True)
+        cast(V, "o00", 0)
+        cast(S, "o00", 1)
+        quant("qd1", 0)
+        quant("o00", 0)
+        quant("qd1", 1)
+        for r in range(4):
+            y_pass(1, 0, r, "state")
+        y_pass(1, 1, 0, "state")
+        cast(S, "o01", 0)
+        cast(S, "o01", 1)
+        decay(1, 1, 0, 0)
+        scores(1, 1, 1, 1)
+        decay(1, 1, 0, 1)
+        decay(1, 1, 1, 0)
+        quant("h11", 0)
+        y_pass(1, 0, 0, 1, stop=True)
+        y_pass(1, 0, 1, 1, stop=True)
+        y_pass(1, 1, 0, 1, stop=True)
+        y_pass(1, 1, 1, 0, start=True, tag="h")
+        y_pass(1, 1, 1, "state")
+        y_pass(1, 1, 1, 1, stop=True)
+        decay(1, 1, 1, 1)
+        quant("o00", 1)
+        store_codes(0, 0)
+        quant("h11", 1)
+        y_pass(1, 0, 2, 1, stop=True)
+        y_pass(1, 0, 3, 1, stop=True)
+        for r in (2, 3):
+            y_pass(1, 1, r, 0, start=True, tag="h")
+            y_pass(1, 1, r, "state")
+            y_pass(1, 1, r, 1, stop=True)
+        for r in range(4):
+            add_bias(1, 0, r)
+            gelu(1, 0, r)
+        store_values(1, 0, every)
+        for r in range(4):
+            add_bias(1, 1, r)
+            gelu(1, 1, r)
+            if r % 2:
+                store_values(1, 1, slice(r - 1, r + 1))
+        quant("o01", 0)
+        quant("o01", 1)
+        store_codes(0, 1)
+        cast(V, "o10", 0)
+        cast(V, "o10", 1)
+        cast(S, "o11", 0)
+        cast(S, "o11", 1)
+        quant("o10", 0)
+        quant("o10", 1)
+        store_codes(1, 0)
+        quant("o11", 0)
+        quant("o11", 1)
+        store_codes(1, 1)
+        for q in range(4):
+            S.dma_start(
+                out=out_2[:, 4 * q : 4 * q + 4, :].bitcast(I32).rearrange("a r w -> r a w"),
+                in_=out_plane[32 * q : 32 * q + 4, :].bitcast(I32).rearrange("p (a w) -> p a w", a=2),
+            )

@@ -22,10 +22,10 @@ HALF = 256
 
 def tile_mix_linattn_tm_pl_gelu_kernel(tc, qc, kc, qd, st, vc_words, vc_scales, dm, b, out_0, out_1, out_2):
     nc = tc.nc
-    V, S = nc.vector, nc.scalar
+    V, S, G = nc.vector, nc.scalar, nc.gpsimd
     with ExitStack() as ctx:
         keep = ctx.enter_context(tc.tile_pool(name="keep", bufs=1))
-        stage = ctx.enter_context(tc.tile_pool(name="stage", bufs=10))
+        stage = ctx.enter_context(tc.tile_pool(name="stage", bufs=7))
         psum = ctx.enter_context(tc.psum_pool(name="psum", bufs=1))
         ctx.enter_context(tc.manual_schedule())
 
@@ -35,7 +35,7 @@ def tile_mix_linattn_tm_pl_gelu_kernel(tc, qc, kc, qd, st, vc_words, vc_scales, 
         raw = {}
 
         def load(name, rows):
-            raw[name] = keep.tile([P, 4, W], F32, name="raw_" + name, tag="raw_" + name)
+            raw[name] = keep.tile([P, 4, rows.shape[1]], F32, name="raw_" + name, tag="raw_" + name)
             nc.sync.dma_start(out=raw[name][:], in_=rows.rearrange("(p j) w -> p j w", j=4))
 
         vc_codes = {}
@@ -53,23 +53,29 @@ def tile_mix_linattn_tm_pl_gelu_kernel(tc, qc, kc, qd, st, vc_words, vc_scales, 
         load("qc0", qc[:, lo])
         b_cols = keep.tile([P, 8], F32)
         S.dma_start(out=b_cols[:].rearrange("p (h c) -> p h c", h=2), in_=b.rearrange("(h p c) -> p h c", h=2, c=4))
-        for q in range(4):
-            S.dma_start(
-                out=vc_plane[32 * q : 32 * q + 4, :].bitcast(I32).rearrange("p (a w) -> p a w", a=2),
-                in_=vc_scales[:, 4 * q : 4 * q + 4, :].bitcast(I32).rearrange("a r w -> r a w"),
-            )
+
+        def load_vc_scales(eng, a):
+            for q in range(4):
+                eng.dma_start(
+                    out=vc_plane[32 * q : 32 * q + 4, M * a : M * (a + 1)].bitcast(I32),
+                    in_=vc_scales[a, 4 * q : 4 * q + 4, :].bitcast(I32),
+                )
+
+        load_vc_scales(S, 0)
         S.activation(out=warm[:], in_=warm[:], func=GELU)
         load("dm00", dm[lo, lo])
-        load("qd0", qd[:, lo])
         load_vc(0)
-        load("st0", st[:, lo])
-        load("st1", st[:, hi])
+        load("st0", st[:, 0:HALF])
+        load("qd0", qd[:, lo])
+        load("st1", st[:, HALF:W])
+        load("st2", st[:, hi])
         load("qc1", qc[:, hi])
         load("dm01", dm[lo, hi])
         load("kc1", kc[:, hi])
         load("qd1", qd[:, hi])
-        load_vc(1)
+        load_vc_scales(nc.sync, 1)
         load("dm11", dm[hi, hi])
+        load_vc(1)
 
         ident = keep.tile([P, P], F32)
         make_identity(nc, ident[:])
@@ -87,42 +93,60 @@ def tile_mix_linattn_tm_pl_gelu_kernel(tc, qc, kc, qd, st, vc_words, vc_scales, 
                 )
 
         staged, codes, scales = {}, {}, {}
+        out_plane = keep.tile([P, 2 * M], U8, align_bytes=64)
+        for name, width in [(n, W) for n in ("kc0", "kc1", "qc0", "qc1", "qd0", "qd1", "h00", "h01", "h11")] + [("st", M), ("o0", M), ("o1", M)]:
+            codes[name] = keep.tile([P, width], U32, name="c_" + name, tag="c_" + name, align_bytes=64)
+            if name[0] == "o":
+                scales[name] = out_plane[:, M * int(name[1]) : M * (int(name[1]) + 1)]
+            else:
+                plane = keep.tile([P, width], U8, name="s_" + name, tag="s_" + name, align_bytes=64)
+                scales[name] = plane[:]
+        values = {}
+        for a in range(2):
+            for n in range(2):
+                part = keep.tile([P, 4, W], F32, name="values%d%d" % (a, n), tag="values%d%d" % (a, n))
+                values[a, n] = part[:]
+        whole = values[0, 0]
 
         def staging(name, g):
-            staged[name, g] = stage.tile([P, 4 * HALF], BF16, name="staged", tag="staged", align_bytes=64)
-            return staged[name, g]
+            if (name, g // 2) not in staged:
+                staged[name, g // 2] = stage.tile([P, 4 * W], BF16, name="staged", tag="staged", align_bytes=64)
+            return staged[name, g // 2][:, 4 * HALF * (g % 2) : 4 * HALF * (g % 2 + 1)]
 
         def pairs(tile, g):
             return tile[:].rearrange("p j (m g s) -> p g m j s", g=2, s=2)[:, g]
 
-        def cast(eng, name, g):
-            dst = staging(name, g)[:]
+        def cast(eng, name, g, part=None):
+            dst = staging(name, g)
             kind = name[:2]
             if kind in ("kc", "qd"):
                 src, dst = pairs(raw[name], g), dst.rearrange("p (s m j) -> p m j s", s=2, j=4)
             elif kind == "qc":
                 src, dst = pairs(raw[name], g), dst.rearrange("p (m s j) -> p m j s", s=2, j=4)
             else:
-                src = raw[name][:, :, HALF * g : HALF * (g + 1)].rearrange("p j (c u) -> p c j u", u=4)
+                if kind == "st":
+                    src = raw["st%d" % g][:] if g < 2 else raw["st2"][:, :, HALF * (g - 2) : HALF * (g - 1)]
+                else:
+                    src = values[int(name[1]), g // 2][:, :, HALF * (g % 2) : HALF * (g % 2 + 1)]
+                if eng is G:
+                    G.tensor_scalar(
+                        out=dst.rearrange("p (w j) -> p w j", j=4), in0=src.rearrange("p j w -> p w j"),
+                        scalar1=1.0, scalar2=-0.0, op0=mybir.AluOpType.mult, op1=mybir.AluOpType.add,
+                    )
+                    return
+                src = src.rearrange("p j (c u) -> p c j u", u=4)
                 dst = dst.rearrange("p (c u j) -> p c j u", u=4, j=4)
+                if part is not None:
+                    src, dst = src[:, 32 * part : 32 * (part + 1)], dst[:, 32 * part : 32 * (part + 1)]
             if eng is V:
                 V.tensor_copy(out=dst, in_=src)
             else:
                 S.copy(out=dst, in_=src)
 
-        out_plane = keep.tile([P, 2 * M], U8, align_bytes=64)
-
-        def quant(name, g):
-            if name not in codes:
-                codes[name] = keep.tile([P, W], U32, name="c_" + name, tag="c_" + name, align_bytes=64)
-                if name[0] == "o":
-                    at = M * int(name[1]) + W * int(name[2])
-                    scales[name] = out_plane[:, at : at + W]
-                else:
-                    plane = keep.tile([P, W], U8, name="s_" + name, tag="s_" + name, align_bytes=64)
-                    scales[name] = plane[:]
-            cols = slice(HALF * g, HALF * (g + 1))
-            V.quantize_mx(out=codes[name][:, cols].bitcast(E4M3), scales=scales[name][:, cols], in_=staged[name, g][:])
+        def quant(name, g, count=1):
+            cols = slice(HALF * g, HALF * (g + count))
+            src = staged[name, g // 2][:, 4 * HALF * (g % 2) : 4 * HALF * (g % 2 + count)]
+            V.quantize_mx(out=codes[name][:, cols].bitcast(E4M3), scales=scales[name][:, cols], in_=src)
 
         score_banks = {}
 
@@ -140,11 +164,9 @@ def tile_mix_linattn_tm_pl_gelu_kernel(tc, qc, kc, qd, st, vc_words, vc_scales, 
 
         def decay(ja, ta, g, u):
             name = "h%d%d" % (ja, ta)
-            if u == 0:
-                staging(name, g)
             ms = slice(64 * u, 64 * (u + 1))
             V.tensor_tensor(
-                out=staged[name, g][:].rearrange("p (s m i) -> p m i s", s=2, i=4)[:, ms],
+                out=staging(name, g).rearrange("p (s m i) -> p m i s", s=2, i=4)[:, ms],
                 in0=score_banks[ja, ta, g, u][:].rearrange("p (i m s) -> p m i s", i=4, s=2),
                 in1=pairs(raw["dm%d%d" % (ja, ta)], g)[:, ms],
                 op=mybir.AluOpType.mult,
@@ -152,41 +174,71 @@ def tile_mix_linattn_tm_pl_gelu_kernel(tc, qc, kc, qd, st, vc_words, vc_scales, 
 
         sums = {}
 
-        def y_pass(a, n, r, part, start=False, stop=False, tag="y"):
-            if start:
-                sums[a, n, r] = bank(tag)
+        def mm(acc, a, r, part, n0, width, start, stop):
             rows = slice(P * r, P * (r + 1))
             if part == "state":
                 left = "qd%d" % a
-                rhs, rhs_scale = codes["st%d" % n][:].bitcast(E4M3), scales["st%d" % n]
+                rhs, rhs_scale = codes["st"][:, n0 : n0 + width].bitcast(E4M3), scales["st"][:, n0 : n0 + width]
             else:
                 left = "h%d%d" % (part, a)
-                rhs = vc_codes[part][:, 2 * W * n : 2 * W * (n + 1)].bitcast(E2M1)
-                rhs_scale = vc_plane[:, M * part + W * n : M * part + W * (n + 1)]
+                rhs = vc_codes[part][:, 2 * n0 : 2 * (n0 + width)].bitcast(E2M1)
+                rhs_scale = vc_plane[:, M * part + n0 : M * part + n0 + width]
             nc.tensor.matmul_mx(
-                out=sums[a, n, r][:], lhsT=codes[left][:, rows].bitcast(E4M3), lhsT_scale=scales[left][:, rows],
+                out=acc, lhsT=codes[left][:, rows].bitcast(E4M3), lhsT_scale=scales[left][:, rows],
                 rhs=rhs, rhs_scale=rhs_scale, start=start, stop=stop,
             )
 
-        def add_bias(a, n, r):
-            name = "o%d%d" % (a, n)
-            if name not in raw:
-                raw[name] = keep.tile([P, 4, W], F32, name="raw_" + name, tag="raw_" + name)
-            V.tensor_tensor(out=raw[name][:, r, :], in0=sums[a, n, r][:], in1=bias[:, W * n : W * (n + 1)], op=mybir.AluOpType.add)
+        def y_pass(a, n, r, part, start=False, stop=False, tag="y"):
+            if start:
+                sums[a, n, r] = bank(tag)
+            mm(sums[a, n, r][:], a, r, part, W * n, W, start, stop)
 
-        def gelu(a, n, r):
-            row = raw["o%d%d" % (a, n)][:, r, :]
-            S.activation(out=row, in_=row, func=GELU)
+        def narrow_values(g, rp):
+            acc = sums["narrow", g, rp] = bank("y")
+            for e in range(2):
+                for c in range(2):
+                    at = HALF * e + P * c
+                    mm(acc[:, at : at + P], 0, 2 * rp + e, 0, HALF * g + P * c, P, e == 0 and c == 0, False)
+
+        def narrow_state(g, rp):
+            acc = sums["narrow", g, rp]
+            for e in range(2):
+                mm(acc[:, HALF * e : HALF * (e + 1)], 0, 2 * rp + e, "state", HALF * g, HALF, False, e == 1)
+
+        def narrow_finish(g, rp):
+            cols = slice(HALF * g, HALF * (g + 1))
+            dst = whole[:, 2 * rp : 2 * rp + 2, cols]
+            V.tensor_tensor(
+                out=dst, in0=sums["narrow", g, rp][:].rearrange("p (e w) -> p e w", e=2),
+                in1=bias[:, cols].unsqueeze(1).to_broadcast([P, 2, HALF]), op=mybir.AluOpType.add,
+            )
+
+        def narrow_gelu(g):
+            dst = whole[:, :, HALF * g : HALF * (g + 1)]
+            S.activation(out=dst, in_=dst, func=GELU)
+
+        def add_bias(a, n, r):
+            V.tensor_tensor(out=values[a, n][:, r, :], in0=sums[a, n, r][:], in1=bias[:, W * n : W * (n + 1)], op=mybir.AluOpType.add)
+
+        def gelu(a, n, rs):
+            rows = values[a, n][:, rs, :]
+            S.activation(out=rows, in_=rows, func=GELU)
 
         def store_values(a, n, rs):
             dst = out_0[W * a : W * (a + 1), W * n : W * (n + 1)].rearrange("(p r) w -> p r w", r=4)
-            nc.sync.dma_start(out=dst[:, rs, :], in_=raw["o%d%d" % (a, n)][:, rs, :])
+            nc.sync.dma_start(out=dst[:, rs, :], in_=values[a, n][:, rs, :])
 
-        def store_codes(a, n):
-            dst = out_1[a].rearrange("p n t -> p (n t)").bitcast(I32)[:, W * n : W * (n + 1)]
-            nc.sync.dma_start(out=dst, in_=codes["o%d%d" % (a, n)][:].bitcast(I32))
+        def store_codes(a, cols):
+            dst = out_1[a].rearrange("p n t -> p (n t)").bitcast(I32)
+            nc.sync.dma_start(out=dst[:, cols], in_=codes["o%d" % a][:, cols].bitcast(I32))
 
-        every = slice(0, 4)
+        def store_scales(eng, a):
+            for q in range(4):
+                eng.dma_start(
+                    out=out_2[a, 4 * q : 4 * q + 4, :].bitcast(I32),
+                    in_=out_plane[32 * q : 32 * q + 4, M * a : M * (a + 1)].bitcast(I32),
+                )
+
 
         for name in ("kc0", "qc0"):
             cast(V, name, 0)
@@ -202,74 +254,85 @@ def tile_mix_linattn_tm_pl_gelu_kernel(tc, qc, kc, qd, st, vc_words, vc_scales, 
         decay(0, 0, 0, 1)
         decay(0, 0, 1, 0)
         quant("h00", 0)
+        narrow_values(0, 0)
+        narrow_values(1, 0)
         decay(0, 0, 1, 1)
-        cast(S, "qd0", 0)
-        cast(S, "qd0", 1)
-        quant("qd0", 0)
+        cast(S, "st", 0)
         quant("h00", 1)
+        narrow_values(0, 1)
+        narrow_values(1, 1)
+        quant("st", 0)
+        cast(V, "qd0", 0)
+        cast(S, "qd0", 1)
+        cast(S, "st", 1)
+        quant("qd0", 0)
+        narrow_state(0, 0)
         quant("qd0", 1)
-        for r in range(4):
-            y_pass(0, 0, r, 0, start=True)
-        cast(V, "st0", 0)
-        cast(S, "st0", 1)
-        quant("st0", 0)
-        quant("st0", 1)
-        for r in range(4):
-            y_pass(0, 0, r, "state", stop=True)
-        cast(S, "st1", 0)
-        cast(S, "st1", 1)
+        narrow_state(0, 1)
         y_pass(0, 1, 0, 0, start=True)
-        for r in range(4):
-            add_bias(0, 0, r)
-            gelu(0, 0, r)
-            if r < 3:
-                y_pass(0, 1, r + 1, 0, start=True)
-        store_values(0, 0, every)
-        quant("st1", 0)
-        quant("st1", 1)
+        narrow_finish(0, 0)
+        quant("st", 1)
+        narrow_state(1, 0)
+        narrow_state(1, 1)
+        narrow_finish(0, 1)
+        y_pass(0, 1, 1, 0, start=True)
+        y_pass(0, 1, 2, 0, start=True)
+        cast(S, "st", 2)
+        narrow_finish(1, 0)
+        cast(V, "st", 3)
+        narrow_finish(1, 1)
+        narrow_gelu(0)
+        y_pass(0, 1, 3, 0, start=True)
+        quant("st", 2, 2)
         for r in range(4):
             y_pass(0, 1, r, "state", stop=True)
         cast(V, "qc1", 0)
         cast(S, "qc1", 1)
+        narrow_gelu(1)
+        store_values(0, 0, slice(0, 4))
         for r in range(4):
             add_bias(0, 1, r)
-            gelu(0, 1, r)
-            if r == 2:
-                quant("qc1", 0)
-                quant("qc1", 1)
+            if r == 0:
+                quant("qc1", 0, 2)
                 scores(0, 1, 0, 0)
                 scores(0, 1, 0, 1)
                 scores(0, 1, 1, 0)
-        store_values(0, 1, every)
+        cast(S, "o0", 0)
+        gelu(0, 1, slice(0, 2))
         cast(S, "kc1", 0)
         cast(S, "kc1", 1)
         cast(S, "qd1", 0)
         cast(S, "qd1", 1)
+        gelu(0, 1, slice(2, 4))
+        store_values(0, 1, slice(0, 4))
         decay(0, 1, 0, 0)
         scores(0, 1, 1, 1)
         decay(0, 1, 0, 1)
         decay(0, 1, 1, 0)
         quant("h01", 0)
+        y_pass(1, 0, 0, 0, start=True)
+        y_pass(1, 0, 1, 0, start=True)
         decay(0, 1, 1, 1)
-        quant("kc1", 0)
-        quant("h01", 1)
-        quant("kc1", 1)
+        cast(V, "o0", 1)
+        quant("kc1", 0, 2)
         scores(1, 1, 0, 0)
         scores(1, 1, 0, 1)
         scores(1, 1, 1, 0)
-        for r in range(4):
-            y_pass(1, 0, r, 0, start=True)
+        quant("h01", 1)
+        y_pass(1, 0, 2, 0, start=True)
+        y_pass(1, 0, 3, 0, start=True)
         y_pass(1, 1, 0, 0, start=True)
-        cast(V, "o00", 0)
-        cast(S, "o00", 1)
+        quant("o0", 0, 2)
+        store_codes(0, lo)
         quant("qd1", 0)
-        quant("o00", 0)
-        quant("qd1", 1)
-        for r in range(4):
-            y_pass(1, 0, r, "state")
+        y_pass(1, 0, 0, "state")
+        y_pass(1, 0, 1, "state")
         y_pass(1, 1, 0, "state")
-        cast(S, "o01", 0)
-        cast(S, "o01", 1)
+        quant("qd1", 1)
+        cast(S, "o0", 2)
+        cast(S, "o0", 3)
+        y_pass(1, 0, 2, "state")
+        y_pass(1, 0, 3, "state")
         decay(1, 1, 0, 0)
         scores(1, 1, 1, 1)
         decay(1, 1, 0, 1)
@@ -278,43 +341,36 @@ def tile_mix_linattn_tm_pl_gelu_kernel(tc, qc, kc, qd, st, vc_words, vc_scales, 
         y_pass(1, 0, 0, 1, stop=True)
         y_pass(1, 0, 1, 1, stop=True)
         y_pass(1, 1, 0, 1, stop=True)
-        y_pass(1, 1, 1, 0, start=True, tag="h")
-        y_pass(1, 1, 1, "state")
-        y_pass(1, 1, 1, 1, stop=True)
         decay(1, 1, 1, 1)
-        quant("o00", 1)
-        store_codes(0, 0)
+        add_bias(1, 0, 0)
+        gelu(1, 0, slice(0, 1))
         quant("h11", 1)
         y_pass(1, 0, 2, 1, stop=True)
         y_pass(1, 0, 3, 1, stop=True)
-        for r in (2, 3):
+        for r in range(1, 4):
             y_pass(1, 1, r, 0, start=True, tag="h")
             y_pass(1, 1, r, "state")
             y_pass(1, 1, r, 1, stop=True)
-        for r in range(4):
+        for r in range(1, 4):
             add_bias(1, 0, r)
-            gelu(1, 0, r)
-        store_values(1, 0, every)
+            gelu(1, 0, slice(r, r + 1))
+            if r == 1:
+                quant("o0", 2, 2)
+                store_codes(0, hi)
+            if r % 2:
+                store_values(1, 0, slice(r - 1, r + 1))
+        store_scales(nc.sync, 0)
         for r in range(4):
             add_bias(1, 1, r)
-            gelu(1, 1, r)
+            gelu(1, 1, slice(r, r + 1))
             if r % 2:
                 store_values(1, 1, slice(r - 1, r + 1))
-        quant("o01", 0)
-        quant("o01", 1)
-        store_codes(0, 1)
-        cast(V, "o10", 0)
-        cast(V, "o10", 1)
-        cast(S, "o11", 0)
-        cast(S, "o11", 1)
-        quant("o10", 0)
-        quant("o10", 1)
-        store_codes(1, 0)
-        quant("o11", 0)
-        quant("o11", 1)
-        store_codes(1, 1)
-        for q in range(4):
-            S.dma_start(
-                out=out_2[:, 4 * q : 4 * q + 4, :].bitcast(I32).rearrange("a r w -> r a w"),
-                in_=out_plane[32 * q : 32 * q + 4, :].bitcast(I32).rearrange("p (a w) -> p a w", a=2),
-            )
+        cast(V, "o1", 0)
+        cast(V, "o1", 1)
+        cast(S, "o1", 3)
+        cast(V, "o1", 2)
+        quant("o1", 0, 2)
+        store_codes(1, lo)
+        quant("o1", 2, 2)
+        store_codes(1, hi)
+        store_scales(S, 1)

@@ -55,10 +55,10 @@ def tile_mix_linattn_tm_pl_gelu_kernel(tc, qc, kc, qd, st, vc_words, vc_scales, 
         S.dma_start(out=b_cols[:].rearrange("p (h c) -> p h c", h=2), in_=b.rearrange("(h p c) -> p h c", h=2, c=4))
 
         def load_vc_scales(eng, a):
-            for q in range(4):
+            for r in range(4):
                 eng.dma_start(
-                    out=vc_plane[32 * q : 32 * q + 4, M * a : M * (a + 1)].bitcast(I32),
-                    in_=vc_scales[a, 4 * q : 4 * q + 4, :].bitcast(I32),
+                    out=vc_plane[r:P:32, M * a : M * (a + 1)].bitcast(I32),
+                    in_=vc_scales[a, r:16:4, :].bitcast(I32),
                 )
 
         load_vc_scales(S, 0)
@@ -232,11 +232,11 @@ def tile_mix_linattn_tm_pl_gelu_kernel(tc, qc, kc, qd, st, vc_words, vc_scales, 
             dst = out_1[a].rearrange("p n t -> p (n t)").bitcast(I32)
             nc.sync.dma_start(out=dst[:, cols], in_=codes["o%d" % a][:, cols].bitcast(I32))
 
-        def store_scales(eng, a):
-            for q in range(4):
-                eng.dma_start(
-                    out=out_2[a, 4 * q : 4 * q + 4, :].bitcast(I32),
-                    in_=out_plane[32 * q : 32 * q + 4, M * a : M * (a + 1)].bitcast(I32),
+        def store_scales(engines, a):
+            for r in range(4):
+                engines[r % len(engines)].dma_start(
+                    out=out_2[a, r:16:4, :].bitcast(I32),
+                    in_=out_plane[r:P:32, M * a : M * (a + 1)].bitcast(I32),
                 )
 
 
@@ -286,18 +286,19 @@ def tile_mix_linattn_tm_pl_gelu_kernel(tc, qc, kc, qd, st, vc_words, vc_scales, 
         quant("st", 2, 2)
         for r in range(4):
             y_pass(0, 1, r, "state", stop=True)
-        cast(V, "qc1", 0)
+        cast(G, "o0", 0)
+        cast(S, "qc1", 0)
         cast(S, "qc1", 1)
         narrow_gelu(1)
         store_values(0, 0, slice(0, 4))
         for r in range(4):
             add_bias(0, 1, r)
-            if r == 0:
+            if r == 1:
                 quant("qc1", 0, 2)
                 scores(0, 1, 0, 0)
                 scores(0, 1, 0, 1)
                 scores(0, 1, 1, 0)
-        cast(S, "o0", 0)
+        cast(G, "o0", 1)
         gelu(0, 1, slice(0, 2))
         cast(S, "kc1", 0)
         cast(S, "kc1", 1)
@@ -313,7 +314,6 @@ def tile_mix_linattn_tm_pl_gelu_kernel(tc, qc, kc, qd, st, vc_words, vc_scales, 
         y_pass(1, 0, 0, 0, start=True)
         y_pass(1, 0, 1, 0, start=True)
         decay(0, 1, 1, 1)
-        cast(V, "o0", 1)
         quant("kc1", 0, 2)
         scores(1, 1, 0, 0)
         scores(1, 1, 0, 1)
@@ -359,13 +359,13 @@ def tile_mix_linattn_tm_pl_gelu_kernel(tc, qc, kc, qd, st, vc_words, vc_scales, 
                 store_codes(0, hi)
             if r % 2:
                 store_values(1, 0, slice(r - 1, r + 1))
-        store_scales(nc.sync, 0)
+        store_scales([nc.sync], 0)
+        cast(G, "o1", 0)
         for r in range(4):
             add_bias(1, 1, r)
             gelu(1, 1, slice(r, r + 1))
             if r % 2:
                 store_values(1, 1, slice(r - 1, r + 1))
-        cast(V, "o1", 0)
         cast(V, "o1", 1)
         cast(S, "o1", 3)
         cast(V, "o1", 2)
@@ -373,4 +373,4 @@ def tile_mix_linattn_tm_pl_gelu_kernel(tc, qc, kc, qd, st, vc_words, vc_scales, 
         store_codes(1, lo)
         quant("o1", 2, 2)
         store_codes(1, hi)
-        store_scales(S, 1)
+        store_scales([S, nc.sync], 1)

@@ -55,26 +55,27 @@ def tile_mix_linattn_tm_pl_gelu_kernel(tc, qc, kc, qd, st, vc_words, vc_scales, 
         S.dma_start(out=b_cols[:].rearrange("p (h c) -> p h c", h=2), in_=b.rearrange("(h p c) -> p h c", h=2, c=4))
 
         def load_vc_scales(eng, a):
-            for r in range(4):
+            for q in range(4):
                 eng.dma_start(
-                    out=vc_plane[r:P:32, M * a : M * (a + 1)].bitcast(I32),
-                    in_=vc_scales[a, r:16:4, :].bitcast(I32),
+                    out=vc_plane[32 * q : 32 * q + 4, M * a : M * (a + 1)].bitcast(I32),
+                    in_=vc_scales[a, 4 * q : 4 * q + 4, :].bitcast(I32),
                 )
 
-        load_vc_scales(S, 0)
         S.activation(out=warm[:], in_=warm[:], func=GELU)
         load("dm00", dm[lo, lo])
-        load_vc(0)
         load("st0", st[:, 0:HALF])
         load("qd0", qd[:, lo])
+        load_vc_scales(nc.sync, 0)
+        load_vc(0)
         load("st1", st[:, HALF:W])
         load("st2", st[:, hi])
         load("qc1", qc[:, hi])
         load("dm01", dm[lo, hi])
         load("kc1", kc[:, hi])
         load("qd1", qd[:, hi])
+        load("dm110", dm[hi, W : W + HALF])
+        load("dm111", dm[hi, W + HALF : 2 * W])
         load_vc_scales(nc.sync, 1)
-        load("dm11", dm[hi, hi])
         load_vc(1)
 
         ident = keep.tile([P, P], F32)
@@ -106,7 +107,6 @@ def tile_mix_linattn_tm_pl_gelu_kernel(tc, qc, kc, qd, st, vc_words, vc_scales, 
             for n in range(2):
                 part = keep.tile([P, 4, W], F32, name="values%d%d" % (a, n), tag="values%d%d" % (a, n))
                 values[a, n] = part[:]
-        whole = values[0, 0]
 
         def staging(name, g):
             if (name, g // 2) not in staged:
@@ -168,7 +168,7 @@ def tile_mix_linattn_tm_pl_gelu_kernel(tc, qc, kc, qd, st, vc_words, vc_scales, 
             V.tensor_tensor(
                 out=staging(name, g).rearrange("p (s m i) -> p m i s", s=2, i=4)[:, ms],
                 in0=score_banks[ja, ta, g, u][:].rearrange("p (i m s) -> p m i s", i=4, s=2),
-                in1=pairs(raw["dm%d%d" % (ja, ta)], g)[:, ms],
+                in1=pairs(raw["dm11%d" % u], g) if ja == 1 else pairs(raw["dm0%d" % ta], g)[:, ms],
                 op=mybir.AluOpType.mult,
             )
 
@@ -193,29 +193,37 @@ def tile_mix_linattn_tm_pl_gelu_kernel(tc, qc, kc, qd, st, vc_words, vc_scales, 
                 sums[a, n, r] = bank(tag)
             mm(sums[a, n, r][:], a, r, part, W * n, W, start, stop)
 
+        def narrow_pass(a, g, rp, part, start=False, stop=False, tag="y"):
+            if start:
+                sums[a, "narrow", g, rp] = bank(tag)
+            acc = sums[a, "narrow", g, rp]
+            width = HALF if part == "state" else P
+            spots = [(e, c) for e in range(2) for c in range(0, HALF, width)]
+            for e, c in spots:
+                at = HALF * e + c
+                mm(acc[:, at : at + width], a, 2 * rp + e, part, HALF * g + c, width, start and (e, c) == spots[0], stop and (e, c) == spots[-1])
+
         def narrow_values(g, rp):
-            acc = sums["narrow", g, rp] = bank("y")
-            for e in range(2):
-                for c in range(2):
-                    at = HALF * e + P * c
-                    mm(acc[:, at : at + P], 0, 2 * rp + e, 0, HALF * g + P * c, P, e == 0 and c == 0, False)
+            narrow_pass(0, g, rp, 0, start=True)
 
         def narrow_state(g, rp):
-            acc = sums["narrow", g, rp]
-            for e in range(2):
-                mm(acc[:, HALF * e : HALF * (e + 1)], 0, 2 * rp + e, "state", HALF * g, HALF, False, e == 1)
+            narrow_pass(0, g, rp, "state", stop=True)
 
-        def narrow_finish(g, rp):
+        def narrow_finish(g, rp, a=0):
             cols = slice(HALF * g, HALF * (g + 1))
-            dst = whole[:, 2 * rp : 2 * rp + 2, cols]
             V.tensor_tensor(
-                out=dst, in0=sums["narrow", g, rp][:].rearrange("p (e w) -> p e w", e=2),
+                out=values[a, g // 2][:, 2 * rp : 2 * rp + 2, HALF * (g % 2) : HALF * (g % 2 + 1)],
+                in0=sums[a, "narrow", g, rp][:].rearrange("p (e w) -> p e w", e=2),
                 in1=bias[:, cols].unsqueeze(1).to_broadcast([P, 2, HALF]), op=mybir.AluOpType.add,
             )
 
-        def narrow_gelu(g):
-            dst = whole[:, :, HALF * g : HALF * (g + 1)]
+        def narrow_gelu(g, a=0, rs=slice(0, 4)):
+            dst = values[a, g // 2][:, rs, HALF * (g % 2) : HALF * (g % 2 + 1)]
             S.activation(out=dst, in_=dst, func=GELU)
+
+        def store_narrow(a, g):
+            dst = out_0[W * a : W * (a + 1), HALF * g : HALF * (g + 1)].rearrange("(p r) w -> p r w", r=4)
+            nc.sync.dma_start(out=dst, in_=values[a, g // 2][:, :, HALF * (g % 2) : HALF * (g % 2 + 1)])
 
         def add_bias(a, n, r):
             V.tensor_tensor(out=values[a, n][:, r, :], in0=sums[a, n, r][:], in1=bias[:, W * n : W * (n + 1)], op=mybir.AluOpType.add)
@@ -254,58 +262,59 @@ def tile_mix_linattn_tm_pl_gelu_kernel(tc, qc, kc, qd, st, vc_words, vc_scales, 
         decay(0, 0, 0, 1)
         decay(0, 0, 1, 0)
         quant("h00", 0)
-        narrow_values(0, 0)
-        narrow_values(1, 0)
         decay(0, 0, 1, 1)
         cast(S, "st", 0)
-        quant("h00", 1)
-        narrow_values(0, 1)
-        narrow_values(1, 1)
         quant("st", 0)
+        quant("h00", 1)
         cast(V, "qd0", 0)
         cast(S, "qd0", 1)
-        cast(S, "st", 1)
         quant("qd0", 0)
+        cast(S, "st", 1)
+        narrow_values(0, 0)
         narrow_state(0, 0)
         quant("qd0", 1)
+        narrow_values(0, 1)
         narrow_state(0, 1)
+        narrow_values(1, 0)
+        narrow_values(1, 1)
         y_pass(0, 1, 0, 0, start=True)
         narrow_finish(0, 0)
+        narrow_finish(0, 1)
         quant("st", 1)
         narrow_state(1, 0)
         narrow_state(1, 1)
-        narrow_finish(0, 1)
         y_pass(0, 1, 1, 0, start=True)
         y_pass(0, 1, 2, 0, start=True)
         cast(S, "st", 2)
-        narrow_finish(1, 0)
         cast(V, "st", 3)
+        narrow_finish(1, 0)
+        quant("st", 2, 2)
         narrow_finish(1, 1)
         narrow_gelu(0)
+        y_pass(0, 1, 0, "state", stop=True)
+        y_pass(0, 1, 1, "state", stop=True)
+        y_pass(0, 1, 2, "state", stop=True)
         y_pass(0, 1, 3, 0, start=True)
-        quant("st", 2, 2)
-        for r in range(4):
-            y_pass(0, 1, r, "state", stop=True)
-        cast(G, "o0", 0)
-        cast(S, "qc1", 0)
+        y_pass(0, 1, 3, "state", stop=True)
+        cast(V, "qc1", 0)
         cast(S, "qc1", 1)
         narrow_gelu(1)
         store_values(0, 0, slice(0, 4))
         for r in range(4):
             add_bias(0, 1, r)
-            if r == 1:
+            if r == 0:
                 quant("qc1", 0, 2)
                 scores(0, 1, 0, 0)
                 scores(0, 1, 0, 1)
                 scores(0, 1, 1, 0)
         cast(G, "o0", 1)
+        cast(G, "o0", 0)
         gelu(0, 1, slice(0, 2))
         cast(S, "kc1", 0)
-        cast(S, "kc1", 1)
-        cast(S, "qd1", 0)
-        cast(S, "qd1", 1)
         gelu(0, 1, slice(2, 4))
         store_values(0, 1, slice(0, 4))
+        cast(S, "qd1", 0)
+        cast(S, "qd1", 1)
         decay(0, 1, 0, 0)
         scores(0, 1, 1, 1)
         decay(0, 1, 0, 1)
@@ -314,63 +323,65 @@ def tile_mix_linattn_tm_pl_gelu_kernel(tc, qc, kc, qd, st, vc_words, vc_scales, 
         y_pass(1, 0, 0, 0, start=True)
         y_pass(1, 0, 1, 0, start=True)
         decay(0, 1, 1, 1)
-        quant("kc1", 0, 2)
-        scores(1, 1, 0, 0)
-        scores(1, 1, 0, 1)
-        scores(1, 1, 1, 0)
+        cast(V, "kc1", 1)
         quant("h01", 1)
         y_pass(1, 0, 2, 0, start=True)
         y_pass(1, 0, 3, 0, start=True)
-        y_pass(1, 1, 0, 0, start=True)
+        quant("kc1", 0, 2)
+        scores(1, 1, 0, 0)
+        scores(1, 1, 1, 0)
+        scores(1, 1, 0, 1)
+        narrow_pass(1, 2, 0, 0, start=True)
         quant("o0", 0, 2)
         store_codes(0, lo)
-        quant("qd1", 0)
-        y_pass(1, 0, 0, "state")
-        y_pass(1, 0, 1, "state")
-        y_pass(1, 1, 0, "state")
-        quant("qd1", 1)
-        cast(S, "o0", 2)
-        cast(S, "o0", 3)
-        y_pass(1, 0, 2, "state")
-        y_pass(1, 0, 3, "state")
         decay(1, 1, 0, 0)
         scores(1, 1, 1, 1)
-        decay(1, 1, 0, 1)
         decay(1, 1, 1, 0)
+        narrow_pass(1, 3, 0, 0, start=True, tag="h")
+        quant("qd1", 0, 2)
+        for r in range(4):
+            y_pass(1, 0, r, "state")
+        narrow_pass(1, 2, 0, "state")
+        narrow_pass(1, 3, 0, "state")
+        cast(S, "o0", 2)
+        cast(S, "o0", 3)
+        decay(1, 1, 0, 1)
+        decay(1, 1, 1, 1)
         quant("h11", 0)
         y_pass(1, 0, 0, 1, stop=True)
         y_pass(1, 0, 1, 1, stop=True)
-        y_pass(1, 1, 0, 1, stop=True)
-        decay(1, 1, 1, 1)
-        add_bias(1, 0, 0)
-        gelu(1, 0, slice(0, 1))
         quant("h11", 1)
         y_pass(1, 0, 2, 1, stop=True)
         y_pass(1, 0, 3, 1, stop=True)
-        for r in range(1, 4):
-            y_pass(1, 1, r, 0, start=True, tag="h")
-            y_pass(1, 1, r, "state")
-            y_pass(1, 1, r, 1, stop=True)
-        for r in range(1, 4):
+        narrow_pass(1, 2, 0, 1, stop=True)
+        narrow_pass(1, 2, 1, 0, start=True, tag="h")
+        narrow_pass(1, 2, 1, "state")
+        narrow_pass(1, 2, 1, 1, stop=True)
+        narrow_pass(1, 3, 0, 1, stop=True)
+        narrow_pass(1, 3, 1, 0, start=True, tag="h")
+        narrow_pass(1, 3, 1, "state")
+        narrow_pass(1, 3, 1, 1, stop=True)
+        quant("o0", 2, 2)
+        store_codes(0, hi)
+        store_scales([nc.sync], 0)
+        for r in range(4):
             add_bias(1, 0, r)
             gelu(1, 0, slice(r, r + 1))
-            if r == 1:
-                quant("o0", 2, 2)
-                store_codes(0, hi)
-            if r % 2:
-                store_values(1, 0, slice(r - 1, r + 1))
-        store_scales([nc.sync], 0)
+            store_values(1, 0, slice(r, r + 1))
         cast(G, "o1", 0)
-        for r in range(4):
-            add_bias(1, 1, r)
-            gelu(1, 1, slice(r, r + 1))
-            if r % 2:
-                store_values(1, 1, slice(r - 1, r + 1))
+        for g in (2, 3):
+            for rp in range(2):
+                narrow_finish(g, rp, 1)
+                narrow_gelu(g, 1, slice(2 * rp, 2 * rp + 2))
+            store_narrow(1, g)
         cast(V, "o1", 1)
-        cast(S, "o1", 3)
         cast(V, "o1", 2)
         quant("o1", 0, 2)
         store_codes(1, lo)
-        quant("o1", 2, 2)
-        store_codes(1, hi)
+        cast(S, "o1", 3, 1)
+        cast(V, "o1", 3, 0)
+        quant("o1", 2)
+        store_codes(1, slice(W, W + HALF))
+        quant("o1", 3)
+        store_codes(1, slice(W + HALF, M))
         store_scales([S, nc.sync], 1)

from contextlib import ExitStack

import concourse.mybir as mybir
from concourse.masks import make_identity

K, M, T = 512, 1024, 1024
FLOPS = 2 * K * T * T + 2 * T * T * M + 2 * K * T * M

F32 = mybir.dt.float32
BF16 = mybir.dt.bfloat16
I32 = mybir.dt.int32
U32 = mybir.dt.uint32
U8 = mybir.dt.uint8
E4M3 = mybir.dt.float8_e4m3fn_x4
E2M1 = mybir.dt.float4_e2m1fn_x4
GELU = mybir.ActivationFunctionType.Gelu_apprx_tanh

P = 128
W = 512
HALF = 256


def tile_mix_linattn_tm_pl_gelu_kernel(tc, qc, kc, qd, st, vc_words, vc_scales, dm, b, out_0, out_1, out_2):
    nc = tc.nc
    V, S, G = nc.vector, nc.scalar, nc.gpsimd
    with ExitStack() as ctx:
        keep = ctx.enter_context(tc.tile_pool(name="keep", bufs=1))
        stage = ctx.enter_context(tc.tile_pool(name="stage", bufs=7))
        psum = ctx.enter_context(tc.psum_pool(name="psum", bufs=1))
        ctx.enter_context(tc.manual_schedule())

        def bank(tag):
            return psum.tile([P, W], F32, name=tag, tag=tag, bufs={"h": 3, "y": 5}[tag])

        raw = {}

        def load(name, rows):
            raw[name] = keep.tile([P, 4, rows.shape[1]], F32, name="raw_" + name, tag="raw_" + name)
            nc.sync.dma_start(out=raw[name][:], in_=rows.rearrange("(p j) w -> p j w", j=4))

        vc_codes = {}

        def load_vc(a):
            vc_codes[a] = keep.tile([P, 2 * M], U8, name="vc%d" % a, tag="vc%d" % a, align_bytes=64)
            nc.sync.dma_start(out=vc_codes[a][:].bitcast(I32), in_=vc_words[a].bitcast(I32))

        lo, hi = slice(0, W), slice(W, 2 * W)
        vc_plane = keep.tile([P, 2 * M], U8, align_bytes=64)
        V.memset(vc_plane[:].bitcast(I32), 0)
        warm = keep.tile([P, 8], F32)
        V.memset(warm[:], 0.0)
        load("kc0", kc[:, lo])
        load("qc0", qc[:, lo])
        b_cols = keep.tile([P, 8], F32)
        S.dma_start(out=b_cols[:].rearrange("p (h c) -> p h c", h=2), in_=b.rearrange("(h p c) -> p h c", h=2, c=4))

        def load_vc_scales(eng, a):
            for q in range(4):
                eng.dma_start(
                    out=vc_plane[32 * q : 32 * q + 4, M * a : M * (a + 1)].bitcast(I32),
                    in_=vc_scales[a, 4 * q : 4 * q + 4, :].bitcast(I32),
                )

        S.activation(out=warm[:], in_=warm[:], func=GELU)
        load("dm00", dm[lo, lo])
        load("st0", st[:, 0:HALF])
        load("qd0", qd[:, lo])
        load_vc_scales(nc.sync, 0)
        load_vc(0)
        load("st1", st[:, HALF:W])
        load("st2", st[:, hi])
        load("qc1", qc[:, hi])
        load("dm01", dm[lo, hi])
        load("kc1", kc[:, hi])
        load("qd1", qd[:, hi])
        load("dm110", dm[hi, W : W + HALF])
        load("dm111", dm[hi, W + HALF : 2 * W])
        load_vc_scales(nc.sync, 1)
        load_vc(1)

        ident = keep.tile([P, P], F32)
        make_identity(nc, ident[:])
        bias = keep.tile([P, M], F32)

        def spread_bias():
            for h in range(2):
                spread = bank("y")
                for c in range(4):
                    col = b_cols[:, 4 * h + c : 4 * h + c + 1]
                    nc.tensor.transpose(spread[:, P * c : P * (c + 1)], col.to_broadcast([P, P]), ident[:])
                S.copy(
                    out=bias[:, W * h : W * (h + 1)].rearrange("p (k c) -> p k c", c=4),
                    in_=spread[:].rearrange("p (c k) -> p k c", c=4),
                )

        staged, codes, scales = {}, {}, {}
        out_plane = keep.tile([P, 2 * M], U8, align_bytes=64)
        for name, width in [(n, W) for n in ("kc0", "kc1", "qc0", "qc1", "qd0", "qd1", "h00", "h01", "h11")] + [("st", M), ("o0", M), ("o1", M)]:
            codes[name] = keep.tile([P, width], U32, name="c_" + name, tag="c_" + name, align_bytes=64)
            if name[0] == "o":
                scales[name] = out_plane[:, M * int(name[1]) : M * (int(name[1]) + 1)]
            else:
                plane = keep.tile([P, width], U8, name="s_" + name, tag="s_" + name, align_bytes=64)
                scales[name] = plane[:]
        values = {}
        for a in range(2):
            for n in range(2):
                part = keep.tile([P, 4, W], F32, name="values%d%d" % (a, n), tag="values%d%d" % (a, n))
                values[a, n] = part[:]

        def staging(name, g):
            if (name, g // 2) not in staged:
                staged[name, g // 2] = stage.tile([P, 4 * W], BF16, name="staged", tag="staged", align_bytes=64)
            return staged[name, g // 2][:, 4 * HALF * (g % 2) : 4 * HALF * (g % 2 + 1)]

        def pairs(tile, g):
            return tile[:].rearrange("p j (m g s) -> p g m j s", g=2, s=2)[:, g]

        def cast(eng, name, g, part=None):
            dst = staging(name, g)
            kind = name[:2]
            if kind in ("kc", "qd"):
                src, dst = pairs(raw[name], g), dst.rearrange("p (s m j) -> p m j s", s=2, j=4)
            elif kind == "qc":
                src, dst = pairs(raw[name], g), dst.rearrange("p (m s j) -> p m j s", s=2, j=4)
            else:
                if kind == "st":
                    src = raw["st%d" % g][:] if g < 2 else raw["st2"][:, :, HALF * (g - 2) : HALF * (g - 1)]
                else:
                    src = values[int(name[1]), g // 2][:, :, HALF * (g % 2) : HALF * (g % 2 + 1)]
                if eng is G:
                    G.tensor_scalar(
                        out=dst.rearrange("p (w j) -> p w j", j=4), in0=src.rearrange("p j w -> p w j"),
                        scalar1=1.0, scalar2=-0.0, op0=mybir.AluOpType.mult, op1=mybir.AluOpType.add,
                    )
                    return
                src = src.rearrange("p j (c u) -> p c j u", u=4)
                dst = dst.rearrange("p (c u j) -> p c j u", u=4, j=4)
                if part is not None:
                    src, dst = src[:, 32 * part : 32 * (part + 1)], dst[:, 32 * part : 32 * (part + 1)]
            if eng is V:
                V.tensor_copy(out=dst, in_=src)
            else:
                S.copy(out=dst, in_=src)

        def quant(name, g, count=1):
            cols = slice(HALF * g, HALF * (g + count))
            src = staged[name, g // 2][:, 4 * HALF * (g % 2) : 4 * HALF * (g % 2 + count)]
            V.quantize_mx(out=codes[name][:, cols].bitcast(E4M3), scales=scales[name][:, cols], in_=src)

        score_banks = {}

        def scores(ja, ta, g, u):
            acc = bank("h")
            score_banks[ja, ta, g, u] = acc
            kn, qn = "kc%d" % ja, "qc%d" % ta
            cols = slice(HALF * g + P * u, HALF * g + P * (u + 1))
            for i in range(4):
                keys = slice(P * i, P * (i + 1))
                nc.tensor.matmul_mx(
                    out=acc[:, keys], lhsT=codes[kn][:, keys].bitcast(E4M3), lhsT_scale=scales[kn][:, keys],
                    rhs=codes[qn][:, cols].bitcast(E4M3), rhs_scale=scales[qn][:, cols], start=True, stop=True,
                )

        def decay(ja, ta, g, u):
            name = "h%d%d" % (ja, ta)
            ms = slice(64 * u, 64 * (u + 1))
            V.tensor_tensor(
                out=staging(name, g).rearrange("p (s m i) -> p m i s", s=2, i=4)[:, ms],
                in0=score_banks[ja, ta, g, u][:].rearrange("p (i m s) -> p m i s", i=4, s=2),
                in1=pairs(raw["dm11%d" % u], g) if ja == 1 else pairs(raw["dm0%d" % ta], g)[:, ms],
                op=mybir.AluOpType.mult,
            )

        sums = {}

        def mm(acc, a, r, part, n0, width, start, stop):
            rows = slice(P * r, P * (r + 1))
            if part == "state":
                left = "qd%d" % a
                rhs, rhs_scale = codes["st"][:, n0 : n0 + width].bitcast(E4M3), scales["st"][:, n0 : n0 + width]
            else:
                left = "h%d%d" % (part, a)
                rhs = vc_codes[part][:, 2 * n0 : 2 * (n0 + width)].bitcast(E2M1)
                rhs_scale = vc_plane[:, M * part + n0 : M * part + n0 + width]
            nc.tensor.matmul_mx(
                out=acc, lhsT=codes[left][:, rows].bitcast(E4M3), lhsT_scale=scales[left][:, rows],
                rhs=rhs, rhs_scale=rhs_scale, start=start, stop=stop,
            )

        def y_pass(a, n, r, part, start=False, stop=False, tag="y"):
            if start:
                sums[a, n, r] = bank(tag)
            mm(sums[a, n, r][:], a, r, part, W * n, W, start, stop)

        def narrow_pass(a, g, rp, part, start=False, stop=False, tag="y"):
            if start:
                sums[a, "narrow", g, rp] = bank(tag)
            acc = sums[a, "narrow", g, rp]
            width = HALF if part == "state" else P
            spots = [(e, c) for e in range(2) for c in range(0, HALF, width)]
            for e, c in spots:
                at = HALF * e + c
                mm(acc[:, at : at + width], a, 2 * rp + e, part, HALF * g + c, width, start and (e, c) == spots[0], stop and (e, c) == spots[-1])

        def narrow_values(g, rp):
            narrow_pass(0, g, rp, 0, start=True)

        def narrow_state(g, rp):
            narrow_pass(0, g, rp, "state", stop=True)

        def narrow_finish(g, rp, a=0):
            cols = slice(HALF * g, HALF * (g + 1))
            V.tensor_tensor(
                out=values[a, g // 2][:, 2 * rp : 2 * rp + 2, HALF * (g % 2) : HALF * (g % 2 + 1)],
                in0=sums[a, "narrow", g, rp][:].rearrange("p (e w) -> p e w", e=2),
                in1=bias[:, cols].unsqueeze(1).to_broadcast([P, 2, HALF]), op=mybir.AluOpType.add,
            )

        def narrow_gelu(g, a=0, rs=slice(0, 4)):
            dst = values[a, g // 2][:, rs, HALF * (g % 2) : HALF * (g % 2 + 1)]
            S.activation(out=dst, in_=dst, func=GELU)

        def store_narrow(a, g):
            dst = out_0[W * a : W * (a + 1), HALF * g : HALF * (g + 1)].rearrange("(p r) w -> p r w", r=4)
            nc.sync.dma_start(out=dst, in_=values[a, g // 2][:, :, HALF * (g % 2) : HALF * (g % 2 + 1)])

        def add_bias(a, n, r):
            V.tensor_tensor(out=values[a, n][:, r, :], in0=sums[a, n, r][:], in1=bias[:, W * n : W * (n + 1)], op=mybir.AluOpType.add)

        def gelu(a, n, rs):
            rows = values[a, n][:, rs, :]
            S.activation(out=rows, in_=rows, func=GELU)

        def store_values(a, n, rs):
            dst = out_0[W * a : W * (a + 1), W * n : W * (n + 1)].rearrange("(p r) w -> p r w", r=4)
            nc.sync.dma_start(out=dst[:, rs, :], in_=values[a, n][:, rs, :])

        def store_codes(a, cols):
            dst = out_1[a].rearrange("p n t -> p (n t)").bitcast(I32)
            nc.sync.dma_start(out=dst[:, cols], in_=codes["o%d" % a][:, cols].bitcast(I32))

        def store_scales(engines, a):
            for r in range(4):
                engines[r % len(engines)].dma_start(
                    out=out_2[a, r:16:4, :].bitcast(I32),
                    in_=out_plane[r:P:32, M * a : M * (a + 1)].bitcast(I32),
                )


        for name in ("kc0", "qc0"):
            cast(V, name, 0)
            cast(S, name, 1)
            quant(name, 0)
            quant(name, 1)
        spread_bias()
        scores(0, 0, 0, 0)
        scores(0, 0, 0, 1)
        scores(0, 0, 1, 0)
        decay(0, 0, 0, 0)
        scores(0, 0, 1, 1)
        decay(0, 0, 0, 1)
        decay(0, 0, 1, 0)
        quant("h00", 0)
        decay(0, 0, 1, 1)
        cast(S, "st", 0)
        quant("st", 0)
        quant("h00", 1)
        cast(V, "qd0", 0)
        cast(S, "qd0", 1)
        quant("qd0", 0)
        cast(S, "st", 1)
        narrow_values(0, 0)
        narrow_state(0, 0)
        quant("qd0", 1)
        narrow_values(0, 1)
        narrow_state(0, 1)
        narrow_values(1, 0)
        narrow_values(1, 1)
        y_pass(0, 1, 0, 0, start=True)
        narrow_finish(0, 0)
        narrow_finish(0, 1)
        quant("st", 1)
        narrow_state(1, 0)
        narrow_state(1, 1)
        y_pass(0, 1, 1, 0, start=True)
        y_pass(0, 1, 2, 0, start=True)
        cast(S, "st", 2)
        cast(V, "st", 3)
        narrow_finish(1, 0)
        quant("st", 2, 2)
        narrow_finish(1, 1)
        narrow_gelu(0)
        y_pass(0, 1, 0, "state", stop=True)
        y_pass(0, 1, 1, "state", stop=True)
        y_pass(0, 1, 2, "state", stop=True)
        y_pass(0, 1, 3, 0, start=True)
        y_pass(0, 1, 3, "state", stop=True)
        cast(V, "qc1", 0)
        cast(S, "qc1", 1)
        narrow_gelu(1)
        store_values(0, 0, slice(0, 4))
        for r in range(4):
            add_bias(0, 1, r)
            if r == 0:
                quant("qc1", 0, 2)
                scores(0, 1, 0, 0)
                scores(0, 1, 0, 1)
                scores(0, 1, 1, 0)
        cast(G, "o0", 1)
        cast(G, "o0", 0)
        gelu(0, 1, slice(0, 2))
        cast(S, "kc1", 0)
        gelu(0, 1, slice(2, 4))
        store_values(0, 1, slice(0, 4))
        cast(S, "qd1", 0)
        cast(S, "qd1", 1)
        decay(0, 1, 0, 0)
        scores(0, 1, 1, 1)
        decay(0, 1, 0, 1)
        decay(0, 1, 1, 0)
        quant("h01", 0)
        y_pass(1, 0, 0, 0, start=True)
        y_pass(1, 0, 1, 0, start=True)
        decay(0, 1, 1, 1)
        cast(V, "kc1", 1)
        quant("h01", 1)
        y_pass(1, 0, 2, 0, start=True)
        y_pass(1, 0, 3, 0, start=True)
        quant("kc1", 0, 2)
        scores(1, 1, 0, 0)
        scores(1, 1, 1, 0)
        scores(1, 1, 0, 1)
        narrow_pass(1, 2, 0, 0, start=True)
        quant("o0", 0, 2)
        store_codes(0, lo)
        decay(1, 1, 0, 0)
        scores(1, 1, 1, 1)
        decay(1, 1, 1, 0)
        narrow_pass(1, 3, 0, 0, start=True, tag="h")
        quant("qd1", 0, 2)
        for r in range(4):
            y_pass(1, 0, r, "state")
        narrow_pass(1, 2, 0, "state")
        narrow_pass(1, 3, 0, "state")
        cast(S, "o0", 2)
        cast(S, "o0", 3)
        decay(1, 1, 0, 1)
        decay(1, 1, 1, 1)
        quant("h11", 0)
        y_pass(1, 0, 0, 1, stop=True)
        y_pass(1, 0, 1, 1, stop=True)
        quant("h11", 1)
        y_pass(1, 0, 2, 1, stop=True)
        y_pass(1, 0, 3, 1, stop=True)
        narrow_pass(1, 2, 0, 1, stop=True)
        narrow_pass(1, 2, 1, 0, start=True, tag="h")
        narrow_pass(1, 2, 1, "state")
        narrow_pass(1, 2, 1, 1, stop=True)
        narrow_pass(1, 3, 0, 1, stop=True)
        narrow_pass(1, 3, 1, 0, start=True, tag="h")
        narrow_pass(1, 3, 1, "state")
        narrow_pass(1, 3, 1, 1, stop=True)
        quant("o0", 2, 2)
        store_codes(0, hi)
        store_scales([nc.sync], 0)
        for r in range(4):
            add_bias(1, 0, r)
            gelu(1, 0, slice(r, r + 1))
            store_values(1, 0, slice(r, r + 1))
        cast(G, "o1", 0)
        for g in (2, 3):
            for rp in range(2):
                narrow_finish(g, rp, 1)
                narrow_gelu(g, 1, slice(2 * rp, 2 * rp + 2))
            store_narrow(1, g)
        cast(V, "o1", 1)
        cast(V, "o1", 2)
        quant("o1", 0, 2)
        store_codes(1, lo)
        cast(S, "o1", 3, 1)
        cast(V, "o1", 3, 0)
        quant("o1", 2)
        store_codes(1, slice(W, W + HALF))
        quant("o1", 3)
        store_codes(1, slice(W + HALF, M))
        store_scales([S, nc.sync], 1)
